import numpy as np
import ml_dtypes


def mxq(x, axis, fmt="e4m3"):
    dtype, down = {"e4m3": (ml_dtypes.float8_e4m3fn, 7), "e5m2": (ml_dtypes.float8_e5m2, 14)}[fmt]
    v = np.moveaxis(np.asarray(x, np.float32).astype(ml_dtypes.bfloat16).astype(np.float64), axis, -1)
    blocks = v.reshape(v.shape[:-1] + (-1, 32))
    amax = np.abs(blocks).max(-1, keepdims=True)
    byte = np.maximum(np.where(amax > 0, np.frexp(amax)[1] - 1 + 127, 0) - down, 1)
    scale = np.exp2(byte - 127.0)
    codes = (blocks / scale).astype(np.float32).astype(dtype).astype(np.float64)
    return np.moveaxis((codes * scale).reshape(v.shape), -1, axis)


WIDE = False


def mx_kscale(k):
    if not WIDE:
        return np.ones(k)
    levels = np.array([10, -10, 5, -5, 0])
    if k % 512:
        return np.exp2(np.random.permutation(np.resize(levels, k // 32))).repeat(32)
    a = np.empty((k // 512, 16))
    for p in range(k // 512):
        a[p, :8] = np.random.permutation(np.resize(levels, 8))
        for g in range(8):
            far = levels[np.abs(levels - a[p, g]) >= 10]
            a[p, g + 8] = far[np.random.randint(len(far))]
    return np.exp2(a.ravel()).repeat(32)


def f64(x):
    return np.asarray(x).astype(np.float64)


def striped(idx):
    return np.tile(idx.reshape(-1, 16).T, (8, 1)).astype(np.uint16)


def unstriped(offs):
    return offs[:16].T.reshape(-1).astype(np.int64)


def pack_weight(w):
    k, n = w.shape
    w = f64(np.asarray(w, np.float32).astype(ml_dtypes.bfloat16)).reshape(k // 32, 32, n)
    amax = np.abs(w).max(1)
    byte = np.clip(np.where(amax > 0, np.frexp(amax)[1] - 1 + 127 - 7, 1), 1, 254)
    scaled = (w * np.exp2(127.0 - byte)[:, None, :]).reshape(k, n).astype(np.float32)
    words = np.ascontiguousarray(scaled.reshape(k // 512, 128, 4, n).transpose(0, 1, 3, 2)).astype(ml_dtypes.float8_e4m3fn).view(np.uint8)
    return words, np.ascontiguousarray(byte.astype(np.uint8).reshape(k // 512, 16, n))


def unpack_weight(words, scales):
    g, p, n, _ = words.shape
    vals = np.ascontiguousarray(words).view(ml_dtypes.float8_e4m3fn).astype(np.float64) * np.repeat(np.exp2(scales.astype(np.float64) - 127.0), 8, axis=1)[..., None]
    return vals.transpose(0, 1, 3, 2).reshape(g * 512, n)


K, T, E, C, N = 1536, 512, 2, 256, 128


def by_expert(wq, xq):
    return np.concatenate([wq[e].T @ xq[:, e * C:(e + 1) * C] for e in range(E)], axis=1)


def setup_inputs():
    n = np.random.standard_normal
    s = mx_kscale(K)[:, None]
    packed = [pack_weight(m) for m in n((E, K, N)) / np.sqrt(K) / s[None]]
    return {
        "xT": (n((K, T)) * s).astype(np.float32),
        "w_words": np.stack([m[0] for m in packed]),
        "w_scales": np.stack([m[1] for m in packed]),
        "gate": np.tile(np.random.uniform(0.2, 1.0, E * C), (N, 1)).astype(np.float32),
        "offs": striped(np.random.permutation(T)[:E * C]),
    }


def reference(xT, w_words, w_scales, gate, offs):
    idx = unstriped(offs)
    xq = mxq(f64(xT)[:, idx], 0, "e4m3")
    w = np.stack([unpack_weight(w_words[e], w_scales[e]) for e in range(E)])
    y = by_expert(w, xq)
    out = np.zeros((N, T))
    out[:, idx] = f64(gate) * y
    return out

@@ -1,0 +1,102 @@
+from contextlib import ExitStack
+
+import concourse.mybir as mybir
+
+K, T, E, C, N = 1536, 512, 2, 256, 128
+FLOPS = 2 * K * N * E * C
+
+F32 = mybir.dt.float32
+BF16 = mybir.dt.bfloat16
+I32 = mybir.dt.int32
+U32 = mybir.dt.uint32
+U16 = mybir.dt.uint16
+U8 = mybir.dt.uint8
+FP8X4 = mybir.dt.float8_e4m3fn_x4
+MULT = mybir.AluOpType.mult
+
+P = 128
+PACK = 4
+PASSES = K // (P * PACK)
+SPLIT = ((160, 160), (512, 64), (512, 112))
+
+
+def tile_routed_moe_kernel(tc, xT, w_words, w_scales, gate, offs, out):
+    nc = tc.nc
+    with ExitStack() as ctx:
+        keep = ctx.enter_context(tc.tile_pool(name="keep", bufs=1))
+        psum = ctx.enter_context(tc.psum_pool(name="psum", bufs=1))
+
+        offsets = keep.tile([P, T // 16], U16, name="offsets")
+        w_codes = keep.tile([P, E, PASSES, N * PACK], U8, name="w_codes", align_bytes=64)
+        w_bytes = keep.tile([P, E * PASSES * N], U8, name="w_bytes", align_bytes=64)
+        gates = keep.tile([P, E * C], F32, name="gates")
+        scales = keep.tile([P, T], U8, name="scales", align_bytes=64)
+        picked_scales = keep.tile([P, E * C], U8, name="picked_scales", align_bytes=64)
+        sums = keep.tile([P, E * C], F32, name="sums")
+        result = keep.tile([P, T], F32, name="result")
+        raw, grouped, words, picked = [], [], [], []
+        for a in range(PASSES):
+            raw.append([keep.tile([P, 2, T], F32, name=f"raw{a}{h}") for h in range(2)])
+            grouped.append(keep.tile([P, T, PACK], BF16, name=f"grouped{a}", align_bytes=64))
+            words.append(keep.tile([P, T], U32, name=f"words{a}", align_bytes=64))
+            picked.append(keep.tile([P, E * C], U32, name=f"picked{a}", align_bytes=64))
+        acc = [psum.tile([N, C], F32, name=f"acc{e}") for e in range(E)]
+
+        nc.gpsimd.memset(scales[:], 0)
+        nc.gpsimd.memset(w_bytes[:], 0)
+
+        x_rows = xT.rearrange("(a p h t) n -> a h p t n", a=PASSES, p=P, h=2)
+        for a in range(PASSES):
+            for h in range(2):
+                nc.sync.dma_start(out=raw[a][h][:], in_=x_rows[a, h])
+                if a == 0 and h == 0:
+                    nc.sync.dma_start(offsets[:], offs)
+        w_rows = w_scales.rearrange("e a q n -> q (e a) n")
+        for q in range(4):
+            nc.sync.dma_start(
+                out=w_bytes[32 * q : 32 * q + 4, :].bitcast(I32).rearrange("q (g n) -> q g n", g=E * PASSES),
+                in_=w_rows[4 * q : 4 * q + 4].bitcast(I32),
+            )
+        nc.sync.dma_start(
+            out=w_codes[:].rearrange("p e a b -> p (e a) b").bitcast(I32),
+            in_=w_words.rearrange("e a p n r -> p (e a) (n r)").bitcast(I32),
+        )
+        nc.sync.dma_start(out=gates[:], in_=gate)
+
+        for a in range(PASSES):
+            for h in range(2):
+                cut = SPLIT[a][h]
+                src = raw[a][h][:].rearrange("p t n -> p n t")
+                dst = grouped[a][:, :, 2 * h : 2 * h + 2]
+                nc.scalar.copy(dst[:, 0:cut, :], src[:, 0:cut, :])
+                if cut < T:
+                    nc.vector.tensor_copy(out=dst[:, cut:T, :], in_=src[:, cut:T, :])
+            nc.vector.quantize_mx(
+                out=words[a][:].bitcast(FP8X4),
+                scales=scales[4 * a : P, :],
+                in_=grouped[a][:].rearrange("p n t -> p (n t)"),
+            )
+            for e in range(E):
+                slots = slice(e * C, (e + 1) * C)
+                listed = offsets[:, e * C // 16 : (e + 1) * C // 16]
+                nc.vector.tensor_copy(out=picked[a][:, slots], in_=words[a][:].indirect(listed))
+                if a == PASSES - 1:
+                    nc.vector.tensor_copy(out=picked_scales[:, slots], in_=scales[:].indirect(listed))
+
+        for e in range(E):
+            slots = slice(e * C, (e + 1) * C)
+            listed = offsets[:, e * C // 16 : (e + 1) * C // 16]
+            for a in range(PASSES):
+                g = e * PASSES + a
+                nc.tensor.matmul_mx(
+                    out=acc[e][:],
+                    lhsT=w_codes[:, e, a, :].bitcast(FP8X4),
+                    lhsT_scale=w_bytes[:, g * N : (g + 1) * N],
+                    rhs=picked[a][:, slots].bitcast(FP8X4),
+                    rhs_scale=picked_scales[4 * a : P, slots],
+                    start=(a == 0),
+                    stop=(a == PASSES - 1),
+                )
+            nc.vector.tensor_tensor(out=sums[:, slots], in0=acc[e][:], in1=gates[:, slots], op=MULT)
+            nc.vector.tensor_copy(out=result[:].indirect(listed), in_=sums[:, slots])
+        nc.sync.dma_start(out=out, in_=result[:])

@@ -17,7 +17,7 @@ MULT = mybir.AluOpType.mult
 P = 128
 PACK = 4
 PASSES = K // (P * PACK)
-SPLIT = ((160, 160), (512, 64), (512, 112))
+SPLIT = (((192, 512), (192, 512)), ((320, 320), (320, 320)), ((352, 352), (208, 352)))
 
 
 def tile_routed_moe_kernel(tc, xT, w_words, w_scales, gate, offs, out):
@@ -32,7 +32,7 @@ def tile_routed_moe_kernel(tc, xT, w_words, w_scales, gate, offs, out):
         gates = keep.tile([P, E * C], F32, name="gates")
         scales = keep.tile([P, T], U8, name="scales", align_bytes=64)
         picked_scales = keep.tile([P, E * C], U8, name="picked_scales", align_bytes=64)
-        sums = keep.tile([P, E * C], F32, name="sums")
+        sums = [keep.tile([P, C], F32, name=f"sums{e}") for e in range(E)]
         result = keep.tile([P, T], F32, name="result")
         raw, grouped, words, picked = [], [], [], []
         for a in range(PASSES):
@@ -49,7 +49,7 @@ def tile_routed_moe_kernel(tc, xT, w_words, w_scales, gate, offs, out):
         for a in range(PASSES):
             for h in range(2):
                 nc.sync.dma_start(out=raw[a][h][:], in_=x_rows[a, h])
-                if a == 0 and h == 0:
+                if a == 0 and h == 1:
                     nc.sync.dma_start(offsets[:], offs)
         w_rows = w_scales.rearrange("e a q n -> q (e a) n")
         for q in range(4):
@@ -63,29 +63,38 @@ def tile_routed_moe_kernel(tc, xT, w_words, w_scales, gate, offs, out):
         )
         nc.sync.dma_start(out=gates[:], in_=gate)
 
-        for a in range(PASSES):
-            for h in range(2):
-                cut = SPLIT[a][h]
-                src = raw[a][h][:].rearrange("p t n -> p n t")
-                dst = grouped[a][:, :, 2 * h : 2 * h + 2]
-                nc.scalar.copy(dst[:, 0:cut, :], src[:, 0:cut, :])
-                if cut < T:
-                    nc.vector.tensor_copy(out=dst[:, cut:T, :], in_=src[:, cut:T, :])
+
+        def part(e):
+            return slice(e * C, (e + 1) * C), offsets[:, e * C // 16 : (e + 1) * C // 16]
+
+        def interleave(a, h):
+            s, g = SPLIT[a][h]
+            src = raw[a][h][:].rearrange("p t n -> p n t")
+            dst = grouped[a][:, :, 2 * h : 2 * h + 2]
+            if s > 0:
+                nc.scalar.copy(dst[:, 0:s, :], src[:, 0:s, :])
+            if g > s:
+                nc.vector.tensor_copy(out=dst[:, s:g, :], in_=src[:, s:g, :])
+            if g < T:
+                nc.gpsimd.tensor_copy(out=dst[:, g:T, :], in_=src[:, g:T, :])
+
+        def quantize(a):
             nc.vector.quantize_mx(
                 out=words[a][:].bitcast(FP8X4),
                 scales=scales[4 * a : P, :],
                 in_=grouped[a][:].rearrange("p n t -> p (n t)"),
             )
-            for e in range(E):
-                slots = slice(e * C, (e + 1) * C)
-                listed = offsets[:, e * C // 16 : (e + 1) * C // 16]
-                nc.vector.tensor_copy(out=picked[a][:, slots], in_=words[a][:].indirect(listed))
-                if a == PASSES - 1:
-                    nc.vector.tensor_copy(out=picked_scales[:, slots], in_=scales[:].indirect(listed))
 
-        for e in range(E):
-            slots = slice(e * C, (e + 1) * C)
-            listed = offsets[:, e * C // 16 : (e + 1) * C // 16]
+        def pick_words(a, e):
+            slots, listed = part(e)
+            nc.vector.tensor_copy(out=picked[a][:, slots], in_=words[a][:].indirect(listed))
+
+        def pick_scales(e):
+            slots, listed = part(e)
+            nc.vector.tensor_copy(out=picked_scales[:, slots], in_=scales[:].indirect(listed))
+
+        def multiply(e):
+            slots, listed = part(e)
             for a in range(PASSES):
                 g = e * PASSES + a
                 nc.tensor.matmul_mx(
@@ -97,6 +106,21 @@ def tile_routed_moe_kernel(tc, xT, w_words, w_scales, gate, offs, out):
                     start=(a == 0),
                     stop=(a == PASSES - 1),
                 )
-            nc.vector.tensor_tensor(out=sums[:, slots], in0=acc[e][:], in1=gates[:, slots], op=MULT)
-            nc.vector.tensor_copy(out=result[:].indirect(listed), in_=sums[:, slots])
+            nc.scalar.copy(sums[e][:], acc[e][:])
+
+        def put_back(e):
+            slots, listed = part(e)
+            nc.vector.tensor_tensor(out=result[:].indirect(listed), in0=sums[e][:], in1=gates[:, slots], op=MULT)
+
+        for a in range(PASSES):
+            interleave(a, 0)
+            interleave(a, 1)
+            quantize(a)
+        for e in range(E):
+            pick_scales(e)
+            for a in range(PASSES):
+                pick_words(a, e)
+            multiply(e)
+        for e in range(E):
+            put_back(e)
         nc.sync.dma_start(out=out, in_=result[:])

@@ -17,7 +17,7 @@ MULT = mybir.AluOpType.mult
 P = 128
 PACK = 4
 PASSES = K // (P * PACK)
-SPLIT = (((192, 512), (192, 512)), ((320, 320), (320, 320)), ((352, 352), (208, 352)))
+SPLIT = (((192, 384), (144, 384)), ((304, 304), (304, 304)), ((336, 336), (240, 336)))
 
 
 def tile_routed_moe_kernel(tc, xT, w_words, w_scales, gate, offs, out):
@@ -37,7 +37,8 @@ def tile_routed_moe_kernel(tc, xT, w_words, w_scales, gate, offs, out):
         raw, grouped, words, picked = [], [], [], []
         for a in range(PASSES):
             raw.append([keep.tile([P, 2, T], F32, name=f"raw{a}{h}") for h in range(2)])
-            grouped.append(keep.tile([P, T, PACK], BF16, name=f"grouped{a}", align_bytes=64))
+            tag = "late" if a == PASSES - 1 else f"grouped{a}"
+            grouped.append(keep.tile([P, T, PACK], BF16, name=f"grouped{a}", tag=tag, align_bytes=64))
             words.append(keep.tile([P, T], U32, name=f"words{a}", align_bytes=64))
             picked.append(keep.tile([P, E * C], U32, name=f"picked{a}", align_bytes=64))
         acc = [psum.tile([N, C], F32, name=f"acc{e}") for e in range(E)]
@@ -85,9 +86,14 @@ def tile_routed_moe_kernel(tc, xT, w_words, w_scales, gate, offs, out):
                 in_=grouped[a][:].rearrange("p n t -> p (n t)"),
             )
 
+        def picked_words(a, e):
+            if e == 1 and a > 0:
+                return picked_late[:, a - 1, :]
+            return picked[a][:, e * C : (e + 1) * C]
+
         def pick_words(a, e):
             slots, listed = part(e)
-            nc.vector.tensor_copy(out=picked[a][:, slots], in_=words[a][:].indirect(listed))
+            nc.vector.tensor_copy(out=picked_words(a, e), in_=words[a][:].indirect(listed))
 
         def pick_scales(e):
             slots, listed = part(e)
@@ -101,7 +107,7 @@ def tile_routed_moe_kernel(tc, xT, w_words, w_scales, gate, offs, out):
                     out=acc[e][:],
                     lhsT=w_codes[:, e, a, :].bitcast(FP8X4),
                     lhsT_scale=w_bytes[:, g * N : (g + 1) * N],
-                    rhs=picked[a][:, slots].bitcast(FP8X4),
+                    rhs=picked_words(a, e).bitcast(FP8X4),
                     rhs_scale=picked_scales[4 * a : P, slots],
                     start=(a == 0),
                     stop=(a == PASSES - 1),
@@ -116,11 +122,17 @@ def tile_routed_moe_kernel(tc, xT, w_words, w_scales, gate, offs, out):
             interleave(a, 0)
             interleave(a, 1)
             quantize(a)
-        for e in range(E):
-            pick_scales(e)
-            for a in range(PASSES):
-                pick_words(a, e)
-            multiply(e)
+        pick_words(0, 0)
+        pick_words(0, 1)
+        pick_words(1, 0)
+        picked_late = keep.tile([P, 2, C], U32, name="picked_late", tag="late", align_bytes=64)
+        pick_scales(0)
+        pick_words(2, 0)
+        multiply(0)
+        pick_scales(1)
+        pick_words(1, 1)
+        pick_words(2, 1)
+        multiply(1)
         for e in range(E):
             put_back(e)
         nc.sync.dma_start(out=out, in_=result[:])

from contextlib import ExitStack

import concourse.mybir as mybir

K, T, E, C, N = 1536, 512, 2, 256, 128
FLOPS = 2 * K * N * E * C

F32 = mybir.dt.float32
BF16 = mybir.dt.bfloat16
I32 = mybir.dt.int32
U32 = mybir.dt.uint32
U16 = mybir.dt.uint16
U8 = mybir.dt.uint8
FP8X4 = mybir.dt.float8_e4m3fn_x4
MULT = mybir.AluOpType.mult

P = 128
PACK = 4
PASSES = K // (P * PACK)
SPLIT = (((192, 384), (144, 384)), ((304, 304), (304, 304)), ((336, 336), (240, 336)))


def tile_routed_moe_kernel(tc, xT, w_words, w_scales, gate, offs, out):
    nc = tc.nc
    with ExitStack() as ctx:
        keep = ctx.enter_context(tc.tile_pool(name="keep", bufs=1))
        psum = ctx.enter_context(tc.psum_pool(name="psum", bufs=1))

        offsets = keep.tile([P, T // 16], U16, name="offsets")
        w_codes = keep.tile([P, E, PASSES, N * PACK], U8, name="w_codes", align_bytes=64)
        w_bytes = keep.tile([P, E * PASSES * N], U8, name="w_bytes", align_bytes=64)
        gates = keep.tile([P, E * C], F32, name="gates")
        scales = keep.tile([P, T], U8, name="scales", align_bytes=64)
        picked_scales = keep.tile([P, E * C], U8, name="picked_scales", align_bytes=64)
        sums = [keep.tile([P, C], F32, name=f"sums{e}") for e in range(E)]
        result = keep.tile([P, T], F32, name="result")
        raw, grouped, words, picked = [], [], [], []
        for a in range(PASSES):
            raw.append([keep.tile([P, 2, T], F32, name=f"raw{a}{h}") for h in range(2)])
            tag = "late" if a == PASSES - 1 else f"grouped{a}"
            grouped.append(keep.tile([P, T, PACK], BF16, name=f"grouped{a}", tag=tag, align_bytes=64))
            words.append(keep.tile([P, T], U32, name=f"words{a}", align_bytes=64))
            picked.append(keep.tile([P, E * C], U32, name=f"picked{a}", align_bytes=64))
        acc = [psum.tile([N, C], F32, name=f"acc{e}") for e in range(E)]

        nc.gpsimd.memset(scales[:], 0)
        nc.gpsimd.memset(w_bytes[:], 0)

        x_rows = xT.rearrange("(a p h t) n -> a h p t n", a=PASSES, p=P, h=2)
        for a in range(PASSES):
            for h in range(2):
                nc.sync.dma_start(out=raw[a][h][:], in_=x_rows[a, h])
                if a == 0 and h == 1:
                    nc.sync.dma_start(offsets[:], offs)
        w_rows = w_scales.rearrange("e a q n -> q (e a) n")
        for q in range(4):
            nc.sync.dma_start(
                out=w_bytes[32 * q : 32 * q + 4, :].bitcast(I32).rearrange("q (g n) -> q g n", g=E * PASSES),
                in_=w_rows[4 * q : 4 * q + 4].bitcast(I32),
            )
        nc.sync.dma_start(
            out=w_codes[:].rearrange("p e a b -> p (e a) b").bitcast(I32),
            in_=w_words.rearrange("e a p n r -> p (e a) (n r)").bitcast(I32),
        )
        nc.sync.dma_start(out=gates[:], in_=gate)


        def part(e):
            return slice(e * C, (e + 1) * C), offsets[:, e * C // 16 : (e + 1) * C // 16]

        def interleave(a, h):
            s, g = SPLIT[a][h]
            src = raw[a][h][:].rearrange("p t n -> p n t")
            dst = grouped[a][:, :, 2 * h : 2 * h + 2]
            if s > 0:
                nc.scalar.copy(dst[:, 0:s, :], src[:, 0:s, :])
            if g > s:
                nc.vector.tensor_copy(out=dst[:, s:g, :], in_=src[:, s:g, :])
            if g < T:
                nc.gpsimd.tensor_copy(out=dst[:, g:T, :], in_=src[:, g:T, :])

        def quantize(a):
            nc.vector.quantize_mx(
                out=words[a][:].bitcast(FP8X4),
                scales=scales[4 * a : P, :],
                in_=grouped[a][:].rearrange("p n t -> p (n t)"),
            )

        def picked_words(a, e):
            if e == 1 and a > 0:
                return picked_late[:, a - 1, :]
            return picked[a][:, e * C : (e + 1) * C]

        def pick_words(a, e):
            slots, listed = part(e)
            nc.vector.tensor_copy(out=picked_words(a, e), in_=words[a][:].indirect(listed))

        def pick_scales(e):
            slots, listed = part(e)
            nc.vector.tensor_copy(out=picked_scales[:, slots], in_=scales[:].indirect(listed))

        def multiply(e):
            slots, listed = part(e)
            for a in range(PASSES):
                g = e * PASSES + a
                nc.tensor.matmul_mx(
                    out=acc[e][:],
                    lhsT=w_codes[:, e, a, :].bitcast(FP8X4),
                    lhsT_scale=w_bytes[:, g * N : (g + 1) * N],
                    rhs=picked_words(a, e).bitcast(FP8X4),
                    rhs_scale=picked_scales[4 * a : P, slots],
                    start=(a == 0),
                    stop=(a == PASSES - 1),
                )
            nc.scalar.copy(sums[e][:], acc[e][:])

        def put_back(e):
            slots, listed = part(e)
            nc.vector.tensor_tensor(out=result[:].indirect(listed), in0=sums[e][:], in1=gates[:, slots], op=MULT)

        for a in range(PASSES):
            interleave(a, 0)
            interleave(a, 1)
            quantize(a)
        pick_words(0, 0)
        pick_words(0, 1)
        pick_words(1, 0)
        picked_late = keep.tile([P, 2, C], U32, name="picked_late", tag="late", align_bytes=64)
        pick_scales(0)
        pick_words(2, 0)
        multiply(0)
        pick_scales(1)
        pick_words(1, 1)
        pick_words(2, 1)
        multiply(1)
        for e in range(E):
            put_back(e)
        nc.sync.dma_start(out=out, in_=result[:])
